import numpy as np
import ml_dtypes


def mxq(x, axis, fmt="e4m3"):
    dtype, down = {"e4m3": (ml_dtypes.float8_e4m3fn, 7), "e5m2": (ml_dtypes.float8_e5m2, 14)}[fmt]
    v = np.moveaxis(np.asarray(x, np.float32).astype(ml_dtypes.bfloat16).astype(np.float64), axis, -1)
    blocks = v.reshape(v.shape[:-1] + (-1, 32))
    amax = np.abs(blocks).max(-1, keepdims=True)
    byte = np.maximum(np.where(amax > 0, np.frexp(amax)[1] - 1 + 127, 0) - down, 1)
    scale = np.exp2(byte - 127.0)
    codes = (blocks / scale).astype(np.float32).astype(dtype).astype(np.float64)
    return np.moveaxis((codes * scale).reshape(v.shape), -1, axis)


WIDE = False


def mx_kscale(k):
    if not WIDE:
        return np.ones(k)
    levels = np.array([10, -10, 5, -5, 0])
    if k % 512:
        return np.exp2(np.random.permutation(np.resize(levels, k // 32))).repeat(32)
    a = np.empty((k // 512, 16))
    for p in range(k // 512):
        a[p, :8] = np.random.permutation(np.resize(levels, 8))
        for g in range(8):
            far = levels[np.abs(levels - a[p, g]) >= 10]
            a[p, g + 8] = far[np.random.randint(len(far))]
    return np.exp2(a.ravel()).repeat(32)


BF16 = ml_dtypes.bfloat16


def bf(x):
    return np.asarray(x, np.float32).astype(BF16)


def f64(x):
    return np.asarray(x).astype(np.float64)


E2M1 = np.array([0.0, 0.5, 1.0, 1.5, 2.0, 3.0, 4.0, 6.0, -0.0, -0.5, -1.0, -1.5, -2.0, -3.0, -4.0, -6.0])


def pack_weight(w, fmt):
    k, n = w.shape
    w = f64(bf(w)).reshape(k // 32, 32, n)
    amax = np.abs(w).max(1)
    if fmt == "e4m3":
        byte = np.frexp(amax)[1] - 1 + 127 - 7
    else:
        mant, ex = np.frexp(amax / 6.0)
        byte = np.where(mant > 0.5, ex, ex - 1) + 127
    byte = np.clip(np.where(amax > 0, byte, 1), 1, 254)
    scaled = (w * np.exp2(127.0 - byte)[:, None, :]).reshape(k, n).astype(np.float32)
    by_word = np.ascontiguousarray(scaled.reshape(k // 512, 128, 4, n).transpose(0, 1, 3, 2))
    if fmt == "e4m3":
        words = by_word.astype(ml_dtypes.float8_e4m3fn).view(np.uint8)
    else:
        c = by_word.astype(ml_dtypes.float4_e2m1fn).view(np.uint8) & 0xF
        words = c[..., 0::2] | (c[..., 1::2] << 4)
    return np.ascontiguousarray(words), np.ascontiguousarray(byte.astype(np.uint8).reshape(k // 512, 16, n))


def unpack_weight(words, scales, fmt):
    g, p, n, _ = words.shape
    if fmt == "e4m3":
        vals = np.ascontiguousarray(words).view(ml_dtypes.float8_e4m3fn).astype(np.float64)
    else:
        nib = np.empty((g, p, n, 4), np.uint8)
        nib[..., 0::2] = words & 0xF
        nib[..., 1::2] = words >> 4
        vals = E2M1[nib]
    vals = vals * np.repeat(np.exp2(scales.astype(np.float64) - 127.0), 8, axis=1)[..., None]
    return vals.transpose(0, 1, 3, 2).reshape(g * 512, n)
def pack4(w):
    words, scales = pack_weight(w, "e2m1")
    return words.reshape(words.shape[0], 128, -1), scales


def unpack4(words, scales):
    return unpack_weight(words.reshape(words.shape[0], 128, -1, 2), scales, "e2m1")


def planes(Y):
    n, m = Y.shape
    b = f64(bf(Y)).reshape(n // 32, 32, m)
    amax = np.abs(b).max(1)
    byte = np.clip(np.where(amax > 0, np.frexp(amax)[1] - 1 + 127 - 7, 1), 1, 254)
    codes = (b * np.exp2(127.0 - byte)[:, None, :]).reshape(n, m).astype(np.float32).astype(ml_dtypes.float8_e4m3fn).view(np.uint8)
    words = codes.reshape(n // 512, 128, 4, m).transpose(0, 1, 3, 2)
    return np.ascontiguousarray(words), np.ascontiguousarray(byte.astype(np.uint8).reshape(n // 512, 16, m))


T, A, F = 2048, 1536, 1024

SHIFT_STD = 0.3
DAY_STD = 0.3
FACTOR_STD = 0.8


def setup_inputs():
    s = mx_kscale(A)
    x = bf(np.random.randn(A, T) * s[:, None])
    x_words, x_scales = pack_weight(f64(x), "e4m3")
    loadings = bf(np.random.randn(A, F) / np.sqrt(A) / s[:, None])
    day_scale = bf(np.exp(DAY_STD * np.random.randn(T)))
    factor_shift = bf(SHIFT_STD * np.random.randn(F))
    factor_scale = bf(np.exp(FACTOR_STD * np.random.randn(F)))
    return {"x_words": x_words, "x_scales": x_scales, "loadings": loadings,
            "day_scale": day_scale, "factor_shift": factor_shift,
            "factor_scale": factor_scale}


def reference(x_words, x_scales, loadings, day_scale, factor_shift, factor_scale):
    X = unpack_weight(x_words, x_scales, "e4m3")
    L = mxq(f64(loadings), 0, "e4m3")
    Z = X.T @ L
    y = np.tanh(Z * f64(day_scale)[:, None] + f64(factor_shift)) * f64(factor_scale)
    Y = y.T
    words, scales = planes(Y)
    return y, words, scales

@@ -1,0 +1,286 @@
+from contextlib import ExitStack
+
+import concourse.mybir as mybir
+from concourse.masks import make_identity
+
+T, A, F = 2048, 1536, 1024
+FLOPS = 2 * T * A * F
+
+F32 = mybir.dt.float32
+BF16 = mybir.dt.bfloat16
+I32 = mybir.dt.int32
+U32 = mybir.dt.uint32
+U8 = mybir.dt.uint8
+FP8X4 = mybir.dt.float8_e4m3fn_x4
+ALU = mybir.AluOpType
+ACT = mybir.ActivationFunctionType
+
+P = 128
+PACK = 4
+K_PASS = P * PACK
+PASSES = A // K_PASS
+HALF = 512
+HALVES = F // HALF
+TILES = T // P
+UNITS = HALVES * TILES
+PAIRS = UNITS // 2
+PAIRS_PER_HALF = TILES // 2
+X_CHUNKS = [(0, 256), (256, 512), (512, 1024), (1024, 1536), (1536, 2048)]
+PLANE_CHUNKS = [(0, 512), (512, 2048)]
+HEAD_SPLIT = 320
+LATE_SPLIT = 192
+
+
+def tile_bounded_factor_signals_planes_g6_kernel(
+    tc, x_words, x_scales, loadings, day_scale, factor_shift, factor_scale, out_0, out_1, out_2
+):
+    nc = tc.nc
+    with ExitStack() as ctx:
+        keep = ctx.enter_context(tc.tile_pool(name="keep", bufs=1))
+        work = ctx.enter_context(tc.tile_pool(name="work", bufs=4))
+        psum = ctx.enter_context(tc.psum_pool(name="psum", bufs=1))
+        ctx.enter_context(tc.manual_schedule())
+
+        x_plane = [
+            keep.tile([P, PASSES, d1 - d0], U8, name="x_plane%d" % d0, align_bytes=64) for d0, d1 in PLANE_CHUNKS
+        ]
+        rows = keep.tile([P, P], BF16, name="rows")
+        cols = keep.tile([P, 32], BF16, name="cols")
+        ident_bf = keep.tile([P, P], BF16, name="ident_bf")
+        ident_f32 = keep.tile([P, P], F32, name="ident_f32")
+        shift_all = keep.tile([P, F], BF16, name="shift_all")
+        warm = keep.tile([P, 8], F32, name="warm")
+        x_code = [
+            keep.tile([P, PASSES, d1 - d0], U32, name="x_code%d" % d0, align_bytes=64) for d0, d1 in X_CHUNKS
+        ]
+        groups = [(h, g) for h in range(HALVES) for g in range(PASSES)]
+        l_raw = {k: keep.tile([P, PACK, HALF], BF16, name="l_raw%d%d" % k, align_bytes=64) for k in groups}
+        l_side = {k: keep.tile([P, HALF, PACK], BF16, name="l_side%d%d" % k, align_bytes=64) for k in groups}
+        l_code = {k: keep.tile([P, HALF], U32, name="l_code%d%d" % k, align_bytes=64) for k in groups}
+        l_plane = {k: keep.tile([P, HALF], U8, name="l_plane%d%d" % k, align_bytes=64) for k in groups}
+        y_code = [keep.tile([P, T], U32, name="y_code%d" % h, align_bytes=64) for h in range(HALVES)]
+        y_plane = [keep.tile([P, T], U8, name="y_plane%d" % h, align_bytes=64) for h in range(HALVES)]
+        scale_all = psum.tile([P, F], BF16, name="scale_all")
+
+        def load_l(h, g):
+            src = loadings[g * K_PASS : (g + 1) * K_PASS, h * HALF : (h + 1) * HALF]
+            nc.sync.dma_start(out=l_raw[h, g][:], in_=src.rearrange("(p j) f -> p j f", j=PACK))
+
+        def load_x(c):
+            d0, d1 = X_CHUNKS[c]
+            src = x_words[:, :, d0:d1, :].rearrange("g p n t -> p g (n t)")
+            nc.sync.dma_start(out=x_code[c][:].bitcast(I32), in_=src.bitcast(I32))
+
+        def load_x_plane(c, queue):
+            d0, d1 = PLANE_CHUNKS[c]
+            for q in range(4):
+                src = x_scales[:, 4 * q : 4 * q + 4, d0:d1].rearrange("g r n -> r g n")
+                queue.dma_start(out=x_plane[c][32 * q : 32 * q + 4, :, :].bitcast(I32), in_=src.bitcast(I32))
+
+        def interleave(copy, h, g, f0, f1):
+            copy(
+                out=l_side[h, g][:, f0:f1, :].rearrange("p (c i) j -> p c j i", i=4),
+                in_=l_raw[h, g][:, :, f0:f1].rearrange("p j (c i) -> p c j i", i=4),
+            )
+
+        def quantize_l(h, g):
+            nc.vector.quantize_mx(
+                out=l_code[h, g][:].bitcast(FP8X4),
+                scales=l_plane[h, g][:],
+                in_=l_side[h, g][:].rearrange("p f j -> p (f j)"),
+            )
+
+        acc, pre, bounded, y_pair, y_bf, turned, y_side = {}, {}, {}, {}, {}, {}, {}
+
+        def one_pass(i, g):
+            h, t = divmod(i, TILES)
+            if g == 0:
+                acc[i] = psum.tile([P, HALF], F32, name="acc", tag="acc", bufs=4)
+            day = t * P
+            c = [n for n, (d0, d1) in enumerate(X_CHUNKS) if d0 <= day < d1][0]
+            off = day - X_CHUNKS[c][0]
+            s = [n for n, (d0, d1) in enumerate(PLANE_CHUNKS) if d0 <= day < d1][0]
+            s_off = day - PLANE_CHUNKS[s][0]
+            nc.tensor.matmul_mx(
+                out=acc[i][:],
+                lhsT=x_code[c][:, g, off : off + P].bitcast(FP8X4),
+                lhsT_scale=x_plane[s][:, g, s_off : s_off + P],
+                rhs=l_code[h, g][:].bitcast(FP8X4),
+                rhs_scale=l_plane[h, g][:],
+                start=(g == 0),
+                stop=(g == PASSES - 1),
+            )
+
+        def multiply(i):
+            for g in range(PASSES):
+                one_pass(i, g)
+
+        def affine(i):
+            h, t = divmod(i, TILES)
+            pre[i] = work.tile([P, HALF], F32, name="pre", tag="pre", bufs=4)
+            nc.vector.scalar_tensor_tensor(
+                out=pre[i][:], in0=acc[i][:], scalar=cols[:, t : t + 1],
+                in1=shift_all[:, h * HALF : (h + 1) * HALF], op0=ALU.mult, op1=ALU.add,
+            )
+            bounded[i] = work.tile([P, HALF], F32, name="bounded", tag="bounded", bufs=4)
+            nc.scalar.activation(out=bounded[i][:], in_=pre[i][:], func=ACT.Tanh)
+
+        def scale(i):
+            h = i // TILES
+            k, e = divmod(i, 2)
+            if e == 0:
+                y_pair[k] = work.tile([P, 2, HALF], F32, name="y_pair", tag="y_pair", bufs=8)
+            nc.vector.tensor_tensor(
+                out=y_pair[k][:, e, :], in0=bounded[i][:], in1=scale_all[:, h * HALF : (h + 1) * HALF], op=ALU.mult
+            )
+
+        def round_y(i, on_vector):
+            k, e = divmod(i, 2)
+            y_bf[i] = work.tile([P, HALF], BF16, name="y_bf", tag="y_bf", bufs=4)
+            dst = y_bf[i][:].rearrange("d (u p e) -> d u p e", u=2, e=2)
+            src = y_pair[k][:, e, :].rearrange("d (p u e) -> d u p e", u=2, e=2)
+            if on_vector:
+                nc.vector.tensor_copy(out=dst, in_=src)
+            else:
+                nc.gpsimd.tensor_scalar(out=dst, in0=src, scalar1=1.0, scalar2=1.0, op0=ALU.mult, op1=ALU.mult)
+
+        def store_y(units):
+            h, t = divmod(units[0], TILES)
+            k, e = divmod(units[0], 2)
+            n = len(units)
+            dst = out_0[t * P : (t + n) * P, h * HALF : (h + 1) * HALF].rearrange("(t p) f -> p t f", p=P)
+            nc.sync.dma_start(out=dst, in_=y_pair[k][:, e : e + n, :])
+
+        def turn(units):
+            bank = psum.tile([P, len(units), 2, P], F32, name="turned", tag="turned", bufs=3)
+            turned[units[0]] = bank
+            for n, i in enumerate(units):
+                words = y_bf[i][:].bitcast(F32)
+                for u in range(2):
+                    nc.tensor.transpose(bank[:, n, u, :], words[:, u * P : (u + 1) * P], ident_f32[:])
+
+        def copy_out(units):
+            n = len(units)
+            side = work.tile([P, n * P * PACK], BF16, name="y_side", tag="y_side", bufs=4, align_bytes=64)
+            y_side[units[0]] = side
+            nc.scalar.copy(
+                out=side[:].bitcast(F32).rearrange("p (n d u) -> p n d u", n=n, u=2),
+                in_=turned[units[0]][:].rearrange("p n u d -> p n d u"),
+            )
+
+        def quantize_y(units):
+            h, t = divmod(units[0], TILES)
+            days = slice(t * P, (t + len(units)) * P)
+            nc.vector.quantize_mx(
+                out=y_code[h][:, days].bitcast(FP8X4), scales=y_plane[h][:, days], in_=y_side[units[0]][:]
+            )
+
+        def store_codes(h, d0, d1):
+            dst = out_1[h, :, d0:d1, :].rearrange("p n t -> p (n t)")
+            nc.sync.dma_start(out=dst.bitcast(I32), in_=y_code[h][:, d0:d1].bitcast(I32))
+
+        def store_scales(h, d0, d1, queues):
+            for q in range(4):
+                queues[q % len(queues)].dma_start(
+                    out=out_2[h, 4 * q : 4 * q + 4, d0:d1].bitcast(I32),
+                    in_=y_plane[h][32 * q : 32 * q + 4, d0:d1].bitcast(I32),
+                )
+
+        def pair(k):
+            return [2 * k, 2 * k + 1]
+
+        nc.scalar.dma_start(out=rows[0:16, :], in_=day_scale.rearrange("(r c) -> r c", c=P))
+        nc.scalar.dma_start(out=rows[16:24, :], in_=factor_shift.rearrange("(r c) -> r c", c=P))
+        nc.scalar.dma_start(out=rows[24:32, :], in_=factor_scale.rearrange("(r c) -> r c", c=P))
+        load_l(0, 0)
+        load_x(0)
+        load_l(0, 1)
+        load_l(0, 2)
+        nc.vector.memset(warm[:], 0.0)
+        nc.scalar.activation(out=warm[:], in_=warm[:], func=ACT.Tanh)
+        make_identity(nc, ident_bf[:])
+        nc.vector.memset(rows[32:64, :], 0.0)
+        nc.vector.memset(rows[64:P, :], 0.0)
+        nc.vector.memset(x_plane[0][:].bitcast(I32), 0)
+        nc.vector.memset(x_plane[1][:].bitcast(I32), 0)
+        nc.vector.tensor_copy(out=ident_f32[:], in_=ident_bf[:])
+        load_x_plane(0, nc.scalar)
+        load_x(1)
+        load_x_plane(1, nc.sync)
+        load_x(2)
+        load_l(1, 0)
+        load_x(3)
+        load_l(1, 1)
+        load_l(1, 2)
+        load_x(4)
+
+        rows_t = psum.tile([P, P], BF16, name="rows_t", tag="turned", bufs=3)
+        nc.tensor.transpose(rows_t[:], rows[:], ident_bf[:])
+        nc.vector.tensor_copy(out=cols[:], in_=rows_t[:, 0:32])
+        shift_ps = psum.tile([P, F], BF16, name="shift_ps", tag="turned", bufs=3)
+        for j in range(F // P):
+            nc.tensor.transpose(
+                shift_ps[:, j * P : (j + 1) * P], cols[:, 16 + j : 17 + j].to_broadcast([P, P]), ident_bf[:]
+            )
+        for j in range(F // P):
+            nc.tensor.transpose(
+                scale_all[:, j * P : (j + 1) * P], cols[:, 24 + j : 25 + j].to_broadcast([P, P]), ident_bf[:]
+            )
+        for g in range(PASSES):
+            interleave(nc.vector.tensor_copy, 0, g, 0, HEAD_SPLIT)
+            interleave(nc.scalar.copy, 0, g, HEAD_SPLIT, HALF)
+            if g == 0:
+                nc.scalar.copy(out=shift_all[:], in_=shift_ps[:])
+            quantize_l(0, g)
+            one_pass(0, g)
+            one_pass(1, g)
+        multiply(2)
+        multiply(3)
+        affine(0)
+        affine(1)
+        interleave(nc.scalar.copy, 1, 0, 0, LATE_SPLIT)
+
+        last = PAIRS - 1
+        for k in range(PAIRS):
+            if k >= 2:
+                quantize_y(pair(k - 2))
+                h, kk = divmod(k - 2, PAIRS_PER_HALF)
+                if kk % 2 == 1:
+                    store_codes(h, (kk - 1) * 2 * P, (kk + 1) * 2 * P)
+                if k - 2 == PAIRS_PER_HALF - 1:
+                    store_scales(0, 0, T, [nc.sync])
+                if k == last - 1:
+                    store_scales(1, 0, T - 6 * P, [nc.sync])
+            if k in (1, 3, 5):
+                interleave(nc.vector.tensor_copy, 1, k // 2, 2 * LATE_SPLIT, HALF)
+            if k in (2, 4, 6):
+                quantize_l(1, k // 2 - 1)
+            if k < last - 1:
+                multiply(2 * k + 4)
+                multiply(2 * k + 5)
+            if k < last:
+                for i in pair(k):
+                    scale(i)
+                    round_y(i, False)
+                store_y(pair(k))
+                turn(pair(k))
+                affine(2 * k + 2)
+                affine(2 * k + 3)
+                copy_out(pair(k))
+                if k <= 4:
+                    g, part = divmod(k + 1, 2)
+                    interleave(nc.scalar.copy, 1, g, part * LATE_SPLIT, (part + 1) * LATE_SPLIT)
+
+        for i in pair(last):
+            scale(i)
+            store_y([i])
+        for i in pair(last):
+            round_y(i, True)
+            turn([i])
+            copy_out([i])
+        quantize_y(pair(last - 1))
+        store_codes(1, T - 4 * P, T - 2 * P)
+        for i in pair(last):
+            quantize_y([i])
+        store_codes(1, T - 2 * P, T)
+        store_scales(1, T - 6 * P, T, [nc.scalar, nc.sync])

@@ -26,8 +26,10 @@ UNITS = HALVES * TILES
 PAIRS = UNITS // 2
 PAIRS_PER_HALF = TILES // 2
 X_CHUNKS = [(0, 256), (256, 512), (512, 1024), (1024, 1536), (1536, 2048)]
+L_LOADS = {(0, 0): [(0, 512)], (0, 1): [(0, 512)], (0, 2): [(0, 256), (256, 512)],
+           (1, 0): [(0, 512)], (1, 1): [(0, 512)], (1, 2): [(0, 512)]}
 PLANE_CHUNKS = [(0, 512), (512, 2048)]
-HEAD_SPLIT = 320
+POOL_COLS = 0
 LATE_SPLIT = 192
 
 
@@ -49,12 +51,17 @@ def tile_bounded_factor_signals_planes_g6_kernel(
         ident_bf = keep.tile([P, P], BF16, name="ident_bf")
         ident_f32 = keep.tile([P, P], F32, name="ident_f32")
         shift_all = keep.tile([P, F], BF16, name="shift_all")
+        scale_sb = keep.tile([P, F], BF16, name="scale_sb")
         warm = keep.tile([P, 8], F32, name="warm")
         x_code = [
             keep.tile([P, PASSES, d1 - d0], U32, name="x_code%d" % d0, align_bytes=64) for d0, d1 in X_CHUNKS
         ]
         groups = [(h, g) for h in range(HALVES) for g in range(PASSES)]
-        l_raw = {k: keep.tile([P, PACK, HALF], BF16, name="l_raw%d%d" % k, align_bytes=64) for k in groups}
+        l_raw = {
+            (h, g, f0): keep.tile([P, PACK, f1 - f0], BF16, name="l_raw%d%d_%d" % (h, g, f0), align_bytes=64)
+            for h, g in groups
+            for f0, f1 in L_LOADS[h, g]
+        }
         l_side = {k: keep.tile([P, HALF, PACK], BF16, name="l_side%d%d" % k, align_bytes=64) for k in groups}
         l_code = {k: keep.tile([P, HALF], U32, name="l_code%d%d" % k, align_bytes=64) for k in groups}
         l_plane = {k: keep.tile([P, HALF], U8, name="l_plane%d%d" % k, align_bytes=64) for k in groups}
@@ -63,8 +70,9 @@ def tile_bounded_factor_signals_planes_g6_kernel(
         scale_all = psum.tile([P, F], BF16, name="scale_all")
 
         def load_l(h, g):
-            src = loadings[g * K_PASS : (g + 1) * K_PASS, h * HALF : (h + 1) * HALF]
-            nc.sync.dma_start(out=l_raw[h, g][:], in_=src.rearrange("(p j) f -> p j f", j=PACK))
+            for f0, f1 in L_LOADS[h, g]:
+                src = loadings[g * K_PASS : (g + 1) * K_PASS, h * HALF + f0 : h * HALF + f1]
+                nc.sync.dma_start(out=l_raw[h, g, f0][:], in_=src.rearrange("(p j) f -> p j f", j=PACK))
 
         def load_x(c):
             d0, d1 = X_CHUNKS[c]
@@ -77,72 +85,91 @@ def tile_bounded_factor_signals_planes_g6_kernel(
                 src = x_scales[:, 4 * q : 4 * q + 4, d0:d1].rearrange("g r n -> r g n")
                 queue.dma_start(out=x_plane[c][32 * q : 32 * q + 4, :, :].bitcast(I32), in_=src.bitcast(I32))
 
-        def interleave(copy, h, g, f0, f1):
-            copy(
-                out=l_side[h, g][:, f0:f1, :].rearrange("p (c i) j -> p c j i", i=4),
-                in_=l_raw[h, g][:, :, f0:f1].rearrange("p j (c i) -> p c j i", i=4),
-            )
+        def gpsimd_copy(out, in_):
+            nc.gpsimd.tensor_scalar(out=out, in0=in_, scalar1=1.0, scalar2=1.0, op0=ALU.mult, op1=ALU.mult)
 
-        def quantize_l(h, g):
+        def interleave(copy, h, g, f0, f1):
+            first = [a for a, b in L_LOADS[h, g] if a <= f0 < b][0]
+            dst = l_side[h, g][:, f0:f1, :]
+            src = l_raw[h, g, first][:, :, f0 - first : f1 - first]
+            if copy is gpsimd_copy:
+                copy(out=dst, in_=src.rearrange("p j f -> p f j"))
+            else:
+                copy(out=dst.rearrange("p (c i) j -> p c j i", i=4), in_=src.rearrange("p j (c i) -> p c j i", i=4))
+
+        def quantize_l(h, g, f0=0, f1=HALF):
             nc.vector.quantize_mx(
-                out=l_code[h, g][:].bitcast(FP8X4),
-                scales=l_plane[h, g][:],
-                in_=l_side[h, g][:].rearrange("p f j -> p (f j)"),
+                out=l_code[h, g][:, f0:f1].bitcast(FP8X4),
+                scales=l_plane[h, g][:, f0:f1],
+                in_=l_side[h, g][:, f0:f1, :].rearrange("p f j -> p (f j)"),
             )
 
         acc, pre, bounded, y_pair, y_bf, turned, y_side = {}, {}, {}, {}, {}, {}, {}
 
-        def one_pass(i, g):
+        def one_pass(i, g, f0=0, f1=HALF):
             h, t = divmod(i, TILES)
             if g == 0:
-                acc[i] = psum.tile([P, HALF], F32, name="acc", tag="acc", bufs=4)
+                acc[i, f0] = psum.tile([P, f1 - f0], F32, name="acc", tag="acc", bufs=4)
             day = t * P
             c = [n for n, (d0, d1) in enumerate(X_CHUNKS) if d0 <= day < d1][0]
             off = day - X_CHUNKS[c][0]
             s = [n for n, (d0, d1) in enumerate(PLANE_CHUNKS) if d0 <= day < d1][0]
             s_off = day - PLANE_CHUNKS[s][0]
             nc.tensor.matmul_mx(
-                out=acc[i][:],
+                out=acc[i, f0][:],
                 lhsT=x_code[c][:, g, off : off + P].bitcast(FP8X4),
                 lhsT_scale=x_plane[s][:, g, s_off : s_off + P],
-                rhs=l_code[h, g][:].bitcast(FP8X4),
-                rhs_scale=l_plane[h, g][:],
+                rhs=l_code[h, g][:, f0:f1].bitcast(FP8X4),
+                rhs_scale=l_plane[h, g][:, f0:f1],
                 start=(g == 0),
                 stop=(g == PASSES - 1),
             )
 
-        def multiply(i):
+        def multiply(i, f0=0, f1=HALF):
             for g in range(PASSES):
-                one_pass(i, g)
+                one_pass(i, g, f0, f1)
 
-        def affine(i):
+        def affine(i, f0=0, f1=HALF):
             h, t = divmod(i, TILES)
-            pre[i] = work.tile([P, HALF], F32, name="pre", tag="pre", bufs=4)
+            if f0 == 0:
+                pre[i] = work.tile([P, HALF], F32, name="pre", tag="pre", bufs=6)
             nc.vector.scalar_tensor_tensor(
-                out=pre[i][:], in0=acc[i][:], scalar=cols[:, t : t + 1],
-                in1=shift_all[:, h * HALF : (h + 1) * HALF], op0=ALU.mult, op1=ALU.add,
+                out=pre[i][:, f0:f1], in0=acc[i, f0][:], scalar=cols[:, t : t + 1],
+                in1=shift_all[:, h * HALF + f0 : h * HALF + f1], op0=ALU.mult, op1=ALU.add,
             )
-            bounded[i] = work.tile([P, HALF], F32, name="bounded", tag="bounded", bufs=4)
-            nc.scalar.activation(out=bounded[i][:], in_=pre[i][:], func=ACT.Tanh)
 
-        def scale(i):
+        def bound(i, f0=0, f1=HALF):
+            if f0 == 0:
+                bounded[i] = work.tile([P, HALF], F32, name="bounded", tag="bounded", bufs=8)
+            nc.scalar.activation(out=bounded[i][:, f0:f1], in_=pre[i][:, f0:f1], func=ACT.Tanh)
+
+        def scale(i, f0=0, f1=HALF, on_gpsimd=False):
             h = i // TILES
             k, e = divmod(i, 2)
-            if e == 0:
+            if k not in y_pair:
                 y_pair[k] = work.tile([P, 2, HALF], F32, name="y_pair", tag="y_pair", bufs=8)
-            nc.vector.tensor_tensor(
-                out=y_pair[k][:, e, :], in0=bounded[i][:], in1=scale_all[:, h * HALF : (h + 1) * HALF], op=ALU.mult
+            engine, factors = (nc.gpsimd, scale_sb) if on_gpsimd else (nc.vector, scale_all)
+            engine.tensor_tensor(
+                out=y_pair[k][:, e, f0:f1], in0=bounded[i][:, f0:f1],
+                in1=factors[:, h * HALF + f0 : h * HALF + f1], op=ALU.mult,
             )
 
-        def round_y(i, on_vector):
+        def round_y(i, copy):
             k, e = divmod(i, 2)
             y_bf[i] = work.tile([P, HALF], BF16, name="y_bf", tag="y_bf", bufs=4)
             dst = y_bf[i][:].rearrange("d (u p e) -> d u p e", u=2, e=2)
             src = y_pair[k][:, e, :].rearrange("d (p u e) -> d u p e", u=2, e=2)
-            if on_vector:
-                nc.vector.tensor_copy(out=dst, in_=src)
-            else:
-                nc.gpsimd.tensor_scalar(out=dst, in0=src, scalar1=1.0, scalar2=1.0, op0=ALU.mult, op1=ALU.mult)
+            copy(out=dst, in_=src)
+
+        def scale_rounded(i):
+            h = i // TILES
+            y_bf[i] = work.tile([P, HALF], BF16, name="y_bf", tag="y_bf", bufs=4)
+            nc.vector.tensor_tensor(
+                out=y_bf[i][:].rearrange("d (u p e) -> d u p e", u=2, e=2),
+                in0=bounded[i][:].rearrange("d (p u e) -> d u p e", u=2, e=2),
+                in1=scale_all[:, h * HALF : (h + 1) * HALF].rearrange("d (p u e) -> d u p e", u=2, e=2),
+                op=ALU.mult,
+            )
 
         def store_y(units):
             h, t = divmod(units[0], TILES)
@@ -159,11 +186,11 @@ def tile_bounded_factor_signals_planes_g6_kernel(
                 for u in range(2):
                     nc.tensor.transpose(bank[:, n, u, :], words[:, u * P : (u + 1) * P], ident_f32[:])
 
-        def copy_out(units):
+        def copy_out(units, copy):
             n = len(units)
             side = work.tile([P, n * P * PACK], BF16, name="y_side", tag="y_side", bufs=4, align_bytes=64)
             y_side[units[0]] = side
-            nc.scalar.copy(
+            copy(
                 out=side[:].bitcast(F32).rearrange("p (n d u) -> p n d u", n=n, u=2),
                 in_=turned[units[0]][:].rearrange("p n u d -> p n d u"),
             )
@@ -193,8 +220,8 @@ def tile_bounded_factor_signals_planes_g6_kernel(
         nc.scalar.dma_start(out=rows[16:24, :], in_=factor_shift.rearrange("(r c) -> r c", c=P))
         nc.scalar.dma_start(out=rows[24:32, :], in_=factor_scale.rearrange("(r c) -> r c", c=P))
         load_l(0, 0)
-        load_x(0)
         load_l(0, 1)
+        load_x(0)
         load_l(0, 2)
         nc.vector.memset(warm[:], 0.0)
         nc.scalar.activation(out=warm[:], in_=warm[:], func=ACT.Tanh)
@@ -205,13 +232,13 @@ def tile_bounded_factor_signals_planes_g6_kernel(
         nc.vector.memset(x_plane[1][:].bitcast(I32), 0)
         nc.vector.tensor_copy(out=ident_f32[:], in_=ident_bf[:])
         load_x_plane(0, nc.scalar)
+        load_l(1, 0)
         load_x(1)
         load_x_plane(1, nc.sync)
         load_x(2)
-        load_l(1, 0)
-        load_x(3)
         load_l(1, 1)
         load_l(1, 2)
+        load_x(3)
         load_x(4)
 
         rows_t = psum.tile([P, P], BF16, name="rows_t", tag="turned", bufs=3)
@@ -227,60 +254,88 @@ def tile_bounded_factor_signals_planes_g6_kernel(
                 scale_all[:, j * P : (j + 1) * P], cols[:, 24 + j : 25 + j].to_broadcast([P, P]), ident_bf[:]
             )
         for g in range(PASSES):
-            interleave(nc.vector.tensor_copy, 0, g, 0, HEAD_SPLIT)
-            interleave(nc.scalar.copy, 0, g, HEAD_SPLIT, HALF)
-            if g == 0:
+            for f0, f1 in L_LOADS[0, g]:
+                cut = f0 + (f1 - f0) * 5 // 8
+                interleave(nc.vector.tensor_copy, 0, g, f0, cut)
+                interleave(nc.scalar.copy, 0, g, cut, f1)
+                quantize_l(0, g, f0, f1)
+            if g == 1:
                 nc.scalar.copy(out=shift_all[:], in_=shift_ps[:])
-            quantize_l(0, g)
+            if g == 1 and POOL_COLS:
+                nc.scalar.copy(out=scale_sb[:], in_=scale_all[:])
             one_pass(0, g)
             one_pass(1, g)
+        interleave(nc.scalar.copy, 1, 0, 0, HALF)
         multiply(2)
         multiply(3)
         affine(0)
+        bound(0)
         affine(1)
-        interleave(nc.scalar.copy, 1, 0, 0, LATE_SPLIT)
+        bound(1)
+        quantize_l(1, 0)
+        multiply(4)
+        affine(2)
+        bound(2)
+        multiply(5)
+        affine(3)
+        bound(3)
 
+        late = {
+            0: [(nc.scalar.copy, 1, 0, 192)],
+            1: [(nc.scalar.copy, 1, 192, 384), (gpsimd_copy, 1, 384, 512)],
+            2: [(nc.scalar.copy, 2, 0, 192)],
+            3: [(nc.scalar.copy, 2, 192, 384), (gpsimd_copy, 2, 384, 512)],
+        }
         last = PAIRS - 1
-        for k in range(PAIRS):
-            if k >= 2:
+        for k in range(last):
+            if k + 3 < PAIRS and k != 5:
+                multiply(2 * k + 6)
+                multiply(2 * k + 7)
+            cut = HALF if k in (1, 3) else HALF - POOL_COLS
+            if cut < HALF:
+                scale(2 * k + 1, cut, HALF, True)
+            scale(2 * k)
+            round_y(2 * k, gpsimd_copy)
+            if 2 <= k < last - 1:
                 quantize_y(pair(k - 2))
                 h, kk = divmod(k - 2, PAIRS_PER_HALF)
                 if kk % 2 == 1:
                     store_codes(h, (kk - 1) * 2 * P, (kk + 1) * 2 * P)
                 if k - 2 == PAIRS_PER_HALF - 1:
                     store_scales(0, 0, T, [nc.sync])
-                if k == last - 1:
-                    store_scales(1, 0, T - 6 * P, [nc.sync])
-            if k in (1, 3, 5):
-                interleave(nc.vector.tensor_copy, 1, k // 2, 2 * LATE_SPLIT, HALF)
-            if k in (2, 4, 6):
-                quantize_l(1, k // 2 - 1)
-            if k < last - 1:
-                multiply(2 * k + 4)
-                multiply(2 * k + 5)
-            if k < last:
-                for i in pair(k):
-                    scale(i)
-                    round_y(i, False)
-                store_y(pair(k))
-                turn(pair(k))
-                affine(2 * k + 2)
-                affine(2 * k + 3)
-                copy_out(pair(k))
-                if k <= 4:
-                    g, part = divmod(k + 1, 2)
-                    interleave(nc.scalar.copy, 1, g, part * LATE_SPLIT, (part + 1) * LATE_SPLIT)
+                if k == last - 2:
+                    store_scales(1, 0, T - 8 * P, [nc.sync])
+            if k in (3, 5):
+                quantize_l(1, k // 2)
+            if k == 5:
+                multiply(2 * k + 6)
+                multiply(2 * k + 7)
+            scale(2 * k + 1, 0, cut)
+            round_y(2 * k + 1, gpsimd_copy)
+            store_y(pair(k))
+            turn(pair(k))
+            if k + 2 < PAIRS:
+                for i in pair(k + 2):
+                    affine(i)
+                    bound(i)
+            for copy, g, c0, c1 in late.get(k, []):
+                interleave(copy, 1, g, c0, c1)
+            copy_out(pair(k), nc.scalar.copy)
 
-        for i in pair(last):
-            scale(i)
-            store_y([i])
-        for i in pair(last):
-            round_y(i, True)
-            turn([i])
-            copy_out([i])
+        i, j = pair(last)
+        for n in (i, j):
+            scale_rounded(n)
+            turn([n])
+            copy_out([n], nc.scalar.copy)
+        scale(i)
+        store_y([i])
+        quantize_y(pair(last - 3))
+        scale(j)
+        store_y([j])
+        quantize_y(pair(last - 2))
+        store_codes(1, T - 8 * P, T - 4 * P)
         quantize_y(pair(last - 1))
-        store_codes(1, T - 4 * P, T - 2 * P)
-        for i in pair(last):
-            quantize_y([i])
-        store_codes(1, T - 2 * P, T)
-        store_scales(1, T - 6 * P, T, [nc.scalar, nc.sync])
+        quantize_y([i])
+        quantize_y([j])
+        store_codes(1, T - 4 * P, T)
+        store_scales(1, T - 8 * P, T, [nc.scalar, nc.sync])

from contextlib import ExitStack

import concourse.mybir as mybir
from concourse.masks import make_identity

T, A, F = 2048, 1536, 1024
FLOPS = 2 * T * A * F

F32 = mybir.dt.float32
BF16 = mybir.dt.bfloat16
I32 = mybir.dt.int32
U32 = mybir.dt.uint32
U8 = mybir.dt.uint8
FP8X4 = mybir.dt.float8_e4m3fn_x4
ALU = mybir.AluOpType
ACT = mybir.ActivationFunctionType

P = 128
PACK = 4
K_PASS = P * PACK
PASSES = A // K_PASS
HALF = 512
HALVES = F // HALF
TILES = T // P
UNITS = HALVES * TILES
PAIRS = UNITS // 2
PAIRS_PER_HALF = TILES // 2
X_CHUNKS = [(0, 256), (256, 512), (512, 1024), (1024, 1536), (1536, 2048)]
L_LOADS = {(0, 0): [(0, 512)], (0, 1): [(0, 512)], (0, 2): [(0, 256), (256, 512)],
           (1, 0): [(0, 512)], (1, 1): [(0, 512)], (1, 2): [(0, 512)]}
PLANE_CHUNKS = [(0, 512), (512, 2048)]
POOL_COLS = 0
LATE_SPLIT = 192


def tile_bounded_factor_signals_planes_g6_kernel(
    tc, x_words, x_scales, loadings, day_scale, factor_shift, factor_scale, out_0, out_1, out_2
):
    nc = tc.nc
    with ExitStack() as ctx:
        keep = ctx.enter_context(tc.tile_pool(name="keep", bufs=1))
        work = ctx.enter_context(tc.tile_pool(name="work", bufs=4))
        psum = ctx.enter_context(tc.psum_pool(name="psum", bufs=1))
        ctx.enter_context(tc.manual_schedule())

        x_plane = [
            keep.tile([P, PASSES, d1 - d0], U8, name="x_plane%d" % d0, align_bytes=64) for d0, d1 in PLANE_CHUNKS
        ]
        rows = keep.tile([P, P], BF16, name="rows")
        cols = keep.tile([P, 32], BF16, name="cols")
        ident_bf = keep.tile([P, P], BF16, name="ident_bf")
        ident_f32 = keep.tile([P, P], F32, name="ident_f32")
        shift_all = keep.tile([P, F], BF16, name="shift_all")
        scale_sb = keep.tile([P, F], BF16, name="scale_sb")
        warm = keep.tile([P, 8], F32, name="warm")
        x_code = [
            keep.tile([P, PASSES, d1 - d0], U32, name="x_code%d" % d0, align_bytes=64) for d0, d1 in X_CHUNKS
        ]
        groups = [(h, g) for h in range(HALVES) for g in range(PASSES)]
        l_raw = {
            (h, g, f0): keep.tile([P, PACK, f1 - f0], BF16, name="l_raw%d%d_%d" % (h, g, f0), align_bytes=64)
            for h, g in groups
            for f0, f1 in L_LOADS[h, g]
        }
        l_side = {k: keep.tile([P, HALF, PACK], BF16, name="l_side%d%d" % k, align_bytes=64) for k in groups}
        l_code = {k: keep.tile([P, HALF], U32, name="l_code%d%d" % k, align_bytes=64) for k in groups}
        l_plane = {k: keep.tile([P, HALF], U8, name="l_plane%d%d" % k, align_bytes=64) for k in groups}
        y_code = [keep.tile([P, T], U32, name="y_code%d" % h, align_bytes=64) for h in range(HALVES)]
        y_plane = [keep.tile([P, T], U8, name="y_plane%d" % h, align_bytes=64) for h in range(HALVES)]
        scale_all = psum.tile([P, F], BF16, name="scale_all")

        def load_l(h, g):
            for f0, f1 in L_LOADS[h, g]:
                src = loadings[g * K_PASS : (g + 1) * K_PASS, h * HALF + f0 : h * HALF + f1]
                nc.sync.dma_start(out=l_raw[h, g, f0][:], in_=src.rearrange("(p j) f -> p j f", j=PACK))

        def load_x(c):
            d0, d1 = X_CHUNKS[c]
            src = x_words[:, :, d0:d1, :].rearrange("g p n t -> p g (n t)")
            nc.sync.dma_start(out=x_code[c][:].bitcast(I32), in_=src.bitcast(I32))

        def load_x_plane(c, queue):
            d0, d1 = PLANE_CHUNKS[c]
            for q in range(4):
                src = x_scales[:, 4 * q : 4 * q + 4, d0:d1].rearrange("g r n -> r g n")
                queue.dma_start(out=x_plane[c][32 * q : 32 * q + 4, :, :].bitcast(I32), in_=src.bitcast(I32))

        def gpsimd_copy(out, in_):
            nc.gpsimd.tensor_scalar(out=out, in0=in_, scalar1=1.0, scalar2=1.0, op0=ALU.mult, op1=ALU.mult)

        def interleave(copy, h, g, f0, f1):
            first = [a for a, b in L_LOADS[h, g] if a <= f0 < b][0]
            dst = l_side[h, g][:, f0:f1, :]
            src = l_raw[h, g, first][:, :, f0 - first : f1 - first]
            if copy is gpsimd_copy:
                copy(out=dst, in_=src.rearrange("p j f -> p f j"))
            else:
                copy(out=dst.rearrange("p (c i) j -> p c j i", i=4), in_=src.rearrange("p j (c i) -> p c j i", i=4))

        def quantize_l(h, g, f0=0, f1=HALF):
            nc.vector.quantize_mx(
                out=l_code[h, g][:, f0:f1].bitcast(FP8X4),
                scales=l_plane[h, g][:, f0:f1],
                in_=l_side[h, g][:, f0:f1, :].rearrange("p f j -> p (f j)"),
            )

        acc, pre, bounded, y_pair, y_bf, turned, y_side = {}, {}, {}, {}, {}, {}, {}

        def one_pass(i, g, f0=0, f1=HALF):
            h, t = divmod(i, TILES)
            if g == 0:
                acc[i, f0] = psum.tile([P, f1 - f0], F32, name="acc", tag="acc", bufs=4)
            day = t * P
            c = [n for n, (d0, d1) in enumerate(X_CHUNKS) if d0 <= day < d1][0]
            off = day - X_CHUNKS[c][0]
            s = [n for n, (d0, d1) in enumerate(PLANE_CHUNKS) if d0 <= day < d1][0]
            s_off = day - PLANE_CHUNKS[s][0]
            nc.tensor.matmul_mx(
                out=acc[i, f0][:],
                lhsT=x_code[c][:, g, off : off + P].bitcast(FP8X4),
                lhsT_scale=x_plane[s][:, g, s_off : s_off + P],
                rhs=l_code[h, g][:, f0:f1].bitcast(FP8X4),
                rhs_scale=l_plane[h, g][:, f0:f1],
                start=(g == 0),
                stop=(g == PASSES - 1),
            )

        def multiply(i, f0=0, f1=HALF):
            for g in range(PASSES):
                one_pass(i, g, f0, f1)

        def affine(i, f0=0, f1=HALF):
            h, t = divmod(i, TILES)
            if f0 == 0:
                pre[i] = work.tile([P, HALF], F32, name="pre", tag="pre", bufs=6)
            nc.vector.scalar_tensor_tensor(
                out=pre[i][:, f0:f1], in0=acc[i, f0][:], scalar=cols[:, t : t + 1],
                in1=shift_all[:, h * HALF + f0 : h * HALF + f1], op0=ALU.mult, op1=ALU.add,
            )

        def bound(i, f0=0, f1=HALF):
            if f0 == 0:
                bounded[i] = work.tile([P, HALF], F32, name="bounded", tag="bounded", bufs=8)
            nc.scalar.activation(out=bounded[i][:, f0:f1], in_=pre[i][:, f0:f1], func=ACT.Tanh)

        def scale(i, f0=0, f1=HALF, on_gpsimd=False):
            h = i // TILES
            k, e = divmod(i, 2)
            if k not in y_pair:
                y_pair[k] = work.tile([P, 2, HALF], F32, name="y_pair", tag="y_pair", bufs=8)
            engine, factors = (nc.gpsimd, scale_sb) if on_gpsimd else (nc.vector, scale_all)
            engine.tensor_tensor(
                out=y_pair[k][:, e, f0:f1], in0=bounded[i][:, f0:f1],
                in1=factors[:, h * HALF + f0 : h * HALF + f1], op=ALU.mult,
            )

        def round_y(i, copy):
            k, e = divmod(i, 2)
            y_bf[i] = work.tile([P, HALF], BF16, name="y_bf", tag="y_bf", bufs=4)
            dst = y_bf[i][:].rearrange("d (u p e) -> d u p e", u=2, e=2)
            src = y_pair[k][:, e, :].rearrange("d (p u e) -> d u p e", u=2, e=2)
            copy(out=dst, in_=src)

        def scale_rounded(i):
            h = i // TILES
            y_bf[i] = work.tile([P, HALF], BF16, name="y_bf", tag="y_bf", bufs=4)
            nc.vector.tensor_tensor(
                out=y_bf[i][:].rearrange("d (u p e) -> d u p e", u=2, e=2),
                in0=bounded[i][:].rearrange("d (p u e) -> d u p e", u=2, e=2),
                in1=scale_all[:, h * HALF : (h + 1) * HALF].rearrange("d (p u e) -> d u p e", u=2, e=2),
                op=ALU.mult,
            )

        def store_y(units):
            h, t = divmod(units[0], TILES)
            k, e = divmod(units[0], 2)
            n = len(units)
            dst = out_0[t * P : (t + n) * P, h * HALF : (h + 1) * HALF].rearrange("(t p) f -> p t f", p=P)
            nc.sync.dma_start(out=dst, in_=y_pair[k][:, e : e + n, :])

        def turn(units):
            bank = psum.tile([P, len(units), 2, P], F32, name="turned", tag="turned", bufs=3)
            turned[units[0]] = bank
            for n, i in enumerate(units):
                words = y_bf[i][:].bitcast(F32)
                for u in range(2):
                    nc.tensor.transpose(bank[:, n, u, :], words[:, u * P : (u + 1) * P], ident_f32[:])

        def copy_out(units, copy):
            n = len(units)
            side = work.tile([P, n * P * PACK], BF16, name="y_side", tag="y_side", bufs=4, align_bytes=64)
            y_side[units[0]] = side
            copy(
                out=side[:].bitcast(F32).rearrange("p (n d u) -> p n d u", n=n, u=2),
                in_=turned[units[0]][:].rearrange("p n u d -> p n d u"),
            )

        def quantize_y(units):
            h, t = divmod(units[0], TILES)
            days = slice(t * P, (t + len(units)) * P)
            nc.vector.quantize_mx(
                out=y_code[h][:, days].bitcast(FP8X4), scales=y_plane[h][:, days], in_=y_side[units[0]][:]
            )

        def store_codes(h, d0, d1):
            dst = out_1[h, :, d0:d1, :].rearrange("p n t -> p (n t)")
            nc.sync.dma_start(out=dst.bitcast(I32), in_=y_code[h][:, d0:d1].bitcast(I32))

        def store_scales(h, d0, d1, queues):
            for q in range(4):
                queues[q % len(queues)].dma_start(
                    out=out_2[h, 4 * q : 4 * q + 4, d0:d1].bitcast(I32),
                    in_=y_plane[h][32 * q : 32 * q + 4, d0:d1].bitcast(I32),
                )

        def pair(k):
            return [2 * k, 2 * k + 1]

        nc.scalar.dma_start(out=rows[0:16, :], in_=day_scale.rearrange("(r c) -> r c", c=P))
        nc.scalar.dma_start(out=rows[16:24, :], in_=factor_shift.rearrange("(r c) -> r c", c=P))
        nc.scalar.dma_start(out=rows[24:32, :], in_=factor_scale.rearrange("(r c) -> r c", c=P))
        load_l(0, 0)
        load_l(0, 1)
        load_x(0)
        load_l(0, 2)
        nc.vector.memset(warm[:], 0.0)
        nc.scalar.activation(out=warm[:], in_=warm[:], func=ACT.Tanh)
        make_identity(nc, ident_bf[:])
        nc.vector.memset(rows[32:64, :], 0.0)
        nc.vector.memset(rows[64:P, :], 0.0)
        nc.vector.memset(x_plane[0][:].bitcast(I32), 0)
        nc.vector.memset(x_plane[1][:].bitcast(I32), 0)
        nc.vector.tensor_copy(out=ident_f32[:], in_=ident_bf[:])
        load_x_plane(0, nc.scalar)
        load_l(1, 0)
        load_x(1)
        load_x_plane(1, nc.sync)
        load_x(2)
        load_l(1, 1)
        load_l(1, 2)
        load_x(3)
        load_x(4)

        rows_t = psum.tile([P, P], BF16, name="rows_t", tag="turned", bufs=3)
        nc.tensor.transpose(rows_t[:], rows[:], ident_bf[:])
        nc.vector.tensor_copy(out=cols[:], in_=rows_t[:, 0:32])
        shift_ps = psum.tile([P, F], BF16, name="shift_ps", tag="turned", bufs=3)
        for j in range(F // P):
            nc.tensor.transpose(
                shift_ps[:, j * P : (j + 1) * P], cols[:, 16 + j : 17 + j].to_broadcast([P, P]), ident_bf[:]
            )
        for j in range(F // P):
            nc.tensor.transpose(
                scale_all[:, j * P : (j + 1) * P], cols[:, 24 + j : 25 + j].to_broadcast([P, P]), ident_bf[:]
            )
        for g in range(PASSES):
            for f0, f1 in L_LOADS[0, g]:
                cut = f0 + (f1 - f0) * 5 // 8
                interleave(nc.vector.tensor_copy, 0, g, f0, cut)
                interleave(nc.scalar.copy, 0, g, cut, f1)
                quantize_l(0, g, f0, f1)
            if g == 1:
                nc.scalar.copy(out=shift_all[:], in_=shift_ps[:])
            if g == 1 and POOL_COLS:
                nc.scalar.copy(out=scale_sb[:], in_=scale_all[:])
            one_pass(0, g)
            one_pass(1, g)
        interleave(nc.scalar.copy, 1, 0, 0, HALF)
        multiply(2)
        multiply(3)
        affine(0)
        bound(0)
        affine(1)
        bound(1)
        quantize_l(1, 0)
        multiply(4)
        affine(2)
        bound(2)
        multiply(5)
        affine(3)
        bound(3)

        late = {
            0: [(nc.scalar.copy, 1, 0, 192)],
            1: [(nc.scalar.copy, 1, 192, 384), (gpsimd_copy, 1, 384, 512)],
            2: [(nc.scalar.copy, 2, 0, 192)],
            3: [(nc.scalar.copy, 2, 192, 384), (gpsimd_copy, 2, 384, 512)],
        }
        last = PAIRS - 1
        for k in range(last):
            if k + 3 < PAIRS and k != 5:
                multiply(2 * k + 6)
                multiply(2 * k + 7)
            cut = HALF if k in (1, 3) else HALF - POOL_COLS
            if cut < HALF:
                scale(2 * k + 1, cut, HALF, True)
            scale(2 * k)
            round_y(2 * k, gpsimd_copy)
            if 2 <= k < last - 1:
                quantize_y(pair(k - 2))
                h, kk = divmod(k - 2, PAIRS_PER_HALF)
                if kk % 2 == 1:
                    store_codes(h, (kk - 1) * 2 * P, (kk + 1) * 2 * P)
                if k - 2 == PAIRS_PER_HALF - 1:
                    store_scales(0, 0, T, [nc.sync])
                if k == last - 2:
                    store_scales(1, 0, T - 8 * P, [nc.sync])
            if k in (3, 5):
                quantize_l(1, k // 2)
            if k == 5:
                multiply(2 * k + 6)
                multiply(2 * k + 7)
            scale(2 * k + 1, 0, cut)
            round_y(2 * k + 1, gpsimd_copy)
            store_y(pair(k))
            turn(pair(k))
            if k + 2 < PAIRS:
                for i in pair(k + 2):
                    affine(i)
                    bound(i)
            for copy, g, c0, c1 in late.get(k, []):
                interleave(copy, 1, g, c0, c1)
            copy_out(pair(k), nc.scalar.copy)

        i, j = pair(last)
        for n in (i, j):
            scale_rounded(n)
            turn([n])
            copy_out([n], nc.scalar.copy)
        scale(i)
        store_y([i])
        quantize_y(pair(last - 3))
        scale(j)
        store_y([j])
        quantize_y(pair(last - 2))
        store_codes(1, T - 8 * P, T - 4 * P)
        quantize_y(pair(last - 1))
        quantize_y([i])
        quantize_y([j])
        store_codes(1, T - 4 * P, T)
        store_scales(1, T - 8 * P, T, [nc.scalar, nc.sync])
